import numpy as np
import ml_dtypes

BF16 = ml_dtypes.bfloat16


def bf(x):
    return np.asarray(x, np.float32).astype(BF16)


def f32(x):
    return np.asarray(x, np.float32)


def f64(x):
    return np.asarray(x).astype(np.float64)


def striped(idx):
    return np.tile(idx.reshape(-1, 16).T, (8, 1))


def rows(idx, k):
    return np.tile(idx, (k, 1))


def look(tab, idx):
    return np.take_along_axis(f64(tab), rows(idx, len(tab)), axis=1)


K, S, D, V, N = 256, 256, 3, 64, 192


def setup_inputs():
    return {"tab": f32(np.random.standard_normal((K, S))), "x0": f32(np.random.standard_normal((K, V))), "offs": striped(np.random.permutation(S)[:N])}


def reference(tab, x0, offs):
    idx = offs[:16].T.reshape(-1)
    x = f64(x0)
    for d in range(D):
        x = np.maximum(x, look(tab, idx[d * V:(d + 1) * V]))
    return x

@@ -1,0 +1,35 @@
+import concourse.mybir as mybir
+
+P = 128
+F32, U16 = mybir.dt.float32, mybir.dt.uint16
+MAX = mybir.AluOpType.max
+
+
+def tile_lookup_pool_max_out_kernel(tc, tab, x0, offs, out):
+    nc = tc.nc
+    rows, width = tab.shape
+    piece = x0.shape[1]
+    columns = piece // 16
+    pieces = offs.shape[1] // columns
+
+    with (
+        tc.tile_pool(name="lists", bufs=1) as lists,
+        tc.tile_pool(name="data", bufs=1) as data,
+    ):
+        offsets = lists.tile([P, offs.shape[1]], U16, name="offsets")
+        nc.sync.dma_start(offsets[:], offs)
+
+        for b in range(rows // P):
+            block = slice(b * P, (b + 1) * P)
+            table = data.tile([P, width], F32, name=f"table{b}")
+            nc.sync.dma_start(table[:], tab[block, :])
+            largest = data.tile([P, piece], F32, name=f"centre{b}")
+            nc.scalar.dma_start(largest[:], x0[block, :])
+
+            for d in range(pieces):
+                neighbour = table[:].indirect(offsets[:, d * columns : (d + 1) * columns])
+                larger = data.tile([P, piece], F32, name=f"largest{b}_{d}")
+                nc.vector.tensor_tensor(larger[:], neighbour, largest[:], MAX)
+                largest = larger
+
+            nc.sync.dma_start(out[block, :], largest[:])

@@ -11,6 +11,11 @@ def tile_lookup_pool_max_out_kernel(tc, tab, x0, offs, out):
     piece = x0.shape[1]
     columns = piece // 16
     pieces = offs.shape[1] // columns
+    blocks = rows // P
+
+    tab_blocks = tab.rearrange("(p b) w -> p b w", b=blocks)
+    x0_rows = x0.rearrange("(p b) v -> p (b v)", b=blocks)
+    out_rows = out.rearrange("(p b) v -> p (b v)", b=blocks)
 
     with (
         tc.tile_pool(name="lists", bufs=1) as lists,
@@ -18,18 +23,18 @@ def tile_lookup_pool_max_out_kernel(tc, tab, x0, offs, out):
     ):
         offsets = lists.tile([P, offs.shape[1]], U16, name="offsets")
         nc.sync.dma_start(offsets[:], offs)
+        largest = data.tile([P, blocks * piece], F32, name="centre")
+        tables = [data.tile([P, width], F32, name=f"table{b}") for b in range(blocks)]
+        nc.scalar.dma_start(tables[0][:], tab_blocks[:, 0, :])
+        nc.scalar.dma_start(largest[:], x0_rows)
+        nc.sync.dma_start(tables[1][:], tab_blocks[:, 1, :])
 
-        for b in range(rows // P):
-            block = slice(b * P, (b + 1) * P)
-            table = data.tile([P, width], F32, name=f"table{b}")
-            nc.sync.dma_start(table[:], tab[block, :])
-            largest = data.tile([P, piece], F32, name=f"centre{b}")
-            nc.scalar.dma_start(largest[:], x0[block, :])
+        for d in range(pieces):
+            larger = data.tile([P, blocks * piece], F32, name=f"largest{d}")
+            for b in range(blocks):
+                neighbour = tables[b][:].indirect(offsets[:, d * columns : (d + 1) * columns])
+                part = slice(b * piece, (b + 1) * piece)
+                nc.vector.tensor_tensor(larger[:, part], neighbour, largest[:, part], MAX)
+            largest = larger
 
-            for d in range(pieces):
-                neighbour = table[:].indirect(offsets[:, d * columns : (d + 1) * columns])
-                larger = data.tile([P, piece], F32, name=f"largest{b}_{d}")
-                nc.vector.tensor_tensor(larger[:], neighbour, largest[:], MAX)
-                largest = larger
-
-            nc.sync.dma_start(out[block, :], largest[:])
+        nc.sync.dma_start(out_rows, largest[:])

import concourse.mybir as mybir

P = 128
F32, U16 = mybir.dt.float32, mybir.dt.uint16
MAX = mybir.AluOpType.max


def tile_lookup_pool_max_out_kernel(tc, tab, x0, offs, out):
    nc = tc.nc
    rows, width = tab.shape
    piece = x0.shape[1]
    columns = piece // 16
    pieces = offs.shape[1] // columns
    blocks = rows // P

    tab_blocks = tab.rearrange("(p b) w -> p b w", b=blocks)
    x0_rows = x0.rearrange("(p b) v -> p (b v)", b=blocks)
    out_rows = out.rearrange("(p b) v -> p (b v)", b=blocks)

    with (
        tc.tile_pool(name="lists", bufs=1) as lists,
        tc.tile_pool(name="data", bufs=1) as data,
    ):
        offsets = lists.tile([P, offs.shape[1]], U16, name="offsets")
        nc.sync.dma_start(offsets[:], offs)
        largest = data.tile([P, blocks * piece], F32, name="centre")
        tables = [data.tile([P, width], F32, name=f"table{b}") for b in range(blocks)]
        nc.scalar.dma_start(tables[0][:], tab_blocks[:, 0, :])
        nc.scalar.dma_start(largest[:], x0_rows)
        nc.sync.dma_start(tables[1][:], tab_blocks[:, 1, :])

        for d in range(pieces):
            larger = data.tile([P, blocks * piece], F32, name=f"largest{d}")
            for b in range(blocks):
                neighbour = tables[b][:].indirect(offsets[:, d * columns : (d + 1) * columns])
                part = slice(b * piece, (b + 1) * piece)
                nc.vector.tensor_tensor(larger[:, part], neighbour, largest[:, part], MAX)
            largest = larger

        nc.sync.dma_start(out_rows, largest[:])
